import numpy as np
import ml_dtypes


def mxq(x, axis, fmt="e4m3"):
    dtype, down = {"e4m3": (ml_dtypes.float8_e4m3fn, 7), "e5m2": (ml_dtypes.float8_e5m2, 14)}[fmt]
    v = np.moveaxis(np.asarray(x, np.float32).astype(ml_dtypes.bfloat16).astype(np.float64), axis, -1)
    blocks = v.reshape(v.shape[:-1] + (-1, 32))
    amax = np.abs(blocks).max(-1, keepdims=True)
    byte = np.maximum(np.where(amax > 0, np.frexp(amax)[1] - 1 + 127, 0) - down, 1)
    scale = np.exp2(byte - 127.0)
    codes = (blocks / scale).astype(np.float32).astype(dtype).astype(np.float64)
    return np.moveaxis((codes * scale).reshape(v.shape), -1, axis)


WIDE = False


def mx_kscale(k):
    if not WIDE:
        return np.ones(k)
    levels = np.array([10, -10, 5, -5, 0])
    if k % 512:
        return np.exp2(np.random.permutation(np.resize(levels, k // 32))).repeat(32)
    a = np.empty((k // 512, 16))
    for p in range(k // 512):
        a[p, :8] = np.random.permutation(np.resize(levels, 8))
        for g in range(8):
            far = levels[np.abs(levels - a[p, g]) >= 10]
            a[p, g + 8] = far[np.random.randint(len(far))]
    return np.exp2(a.ravel()).repeat(32)


def f64(x):
    return np.asarray(x).astype(np.float64)


def striped(idx):
    return np.tile(idx.reshape(-1, 16).T, (8, 1)).astype(np.uint16)


def unstriped(offs):
    return offs[:16].T.reshape(-1).astype(np.int64)


def silu(v):
    return v / (1.0 + np.exp(-np.maximum(v, -700.0)))


K, T, E, C, H, N = 512, 1536, 6, 128, 1024, 256


def by_expert(wq, xq):
    return np.concatenate([wq[e].T @ xq[:, e * C:(e + 1) * C] for e in range(E)], axis=1)


def setup_inputs():
    n = np.random.standard_normal
    s = mx_kscale(K)[:, None]
    u = mx_kscale(H)
    return {
        "xT": (n((K, T)) * s).astype(np.float32),
        "w1": (n((E, K, H)) / np.sqrt(K) / s[None] * u[None, None, :]).astype(np.float32),
        "w2": (n((E, H, N)) / np.sqrt(H) / u[None, :, None]).astype(np.float32),
        "gate": np.tile(np.random.uniform(0.2, 1.0, E * C), (K, 1)).astype(np.float32),
        "offs": striped(np.random.permutation(T)[:E * C]),
    }


def reference(xT, w1, w2, gate, offs):
    idx = unstriped(offs)
    xq = mxq(f64(gate) * f64(xT)[:, idx], 0, "e4m3")
    h = silu(by_expert(mxq(f64(w1), 1, "e4m3"), xq))
    y = by_expert(mxq(f64(w2), 1, "e4m3"), mxq(h, 0, "e4m3"))
    out = np.zeros((N, T))
    out[:, idx] = y
    return out

@@ -1,0 +1,255 @@
+from contextlib import ExitStack
+
+import concourse.mybir as mybir
+
+K, T, E, C, H, N = 512, 1536, 6, 128, 1024, 256
+S = E * C
+FLOPS = 2 * S * (K * H + H * N)
+
+F32 = mybir.dt.float32
+BF16 = mybir.dt.bfloat16
+U32 = mybir.dt.uint32
+U16 = mybir.dt.uint16
+U8 = mybir.dt.uint8
+FP8X4 = mybir.dt.float8_e4m3fn_x4
+MULT = mybir.AluOpType.mult
+SILU = mybir.ActivationFunctionType.Silu
+
+P = 128
+PACK = 4
+K_PASS = P * PACK
+H_PASSES = H // K_PASS
+N_HALVES = N // P
+CHUNK = 2 * C
+ALIGN = 64
+KIB = 1024
+W1_SLOT = 16 * KIB
+W2_SLOT = 8 * KIB
+GATE_AT = E * W1_SLOT
+W2_AT = GATE_AT + 12 * KIB
+W2_SLOTS = E - 1
+
+
+def tile_moe_pre_mlp_silu_kernel(tc, xT, w1, w2, gate, offs, out):
+    nc = tc.nc
+    with ExitStack() as ctx:
+        held = ctx.enter_context(tc.tile_pool(name="held", bufs=1))
+        cols = ctx.enter_context(tc.tile_pool(name="cols", bufs=4))
+        arena = ctx.enter_context(tc.tile_pool(name="arena", bufs=1))
+        stage = ctx.enter_context(tc.tile_pool(name="stage", bufs=2))
+        psum = ctx.enter_context(tc.psum_pool(name="psum", bufs=2))
+
+        offsets = held.tile([P, S // 16], U16, name="offsets")
+        nc.sync.dma_start(offsets[:], offs)
+
+        gate_sb = arena.tile([P, PACK, S], F32, name="gate_sb", align_bytes=ALIGN, offset=GATE_AT)
+        nc.sync.dma_start(out=gate_sb[:], in_=gate.rearrange("(p j) s -> p j s", j=PACK))
+        x_rows = xT.rearrange("(p j) t -> p j t", j=PACK)
+        x_sb = []
+        for j in range(PACK):
+            tile = cols.tile([P, T], F32, name="x_sb", tag="cols")
+            nc.sync.dma_start(out=tile[:], in_=x_rows[:, j, :])
+            x_sb.append(tile)
+
+        w1_raw = {}
+        w2_raw = {}
+
+        def load_w1(e):
+            tile = arena.tile([P, PACK, H], F32, name=f"w1_raw{e}", align_bytes=ALIGN, offset=e * W1_SLOT)
+            nc.sync.dma_start(out=tile[:], in_=w1[e].rearrange("(p j) i -> p j i", j=PACK))
+            w1_raw[e] = tile
+
+        def load_w2(e):
+            tile = arena.tile(
+                [P, H_PASSES, PACK, N], F32, name=f"w2_raw{e}", align_bytes=ALIGN, offset=W2_AT + (e % W2_SLOTS) * W2_SLOT
+            )
+            rows = w2[e].rearrange("(g p j) n -> p g (j n)", g=H_PASSES, j=PACK)
+            if e < E - 1:
+                nc.sync.dma_start(out=tile[:].rearrange("p g j n -> p g (j n)"), in_=rows)
+            else:
+                for g in range(H_PASSES):
+                    nc.sync.dma_start(out=tile[:, g, :, :].rearrange("p j n -> p (j n)"), in_=rows[:, g, :])
+            w2_raw[e] = tile
+
+        for e in range(E - 2):
+            load_w1(e)
+            load_w2(e)
+        load_w1(E - 2)
+        load_w1(E - 1)
+        load_w2(E - 2)
+        load_w2(E - 1)
+
+        windows = []
+        for half in range(N_HALVES):
+            tile = held.tile([P, T], F32, name=f"window{half}")
+            nc.gpsimd.memset(tile[:], 0.0)
+            windows.append(tile)
+
+        def copy_on(engine, dst, src):
+            if engine == "vector":
+                nc.vector.tensor_copy(out=dst, in_=src)
+            else:
+                nc.scalar.copy(out=dst, in_=src)
+
+        def quantize(src, words, name, bufs):
+            codes = stage.tile([P, words], U32, name=name + "_codes", align_bytes=ALIGN, bufs=bufs)
+            scales = stage.tile([P, words], U8, name=name + "_scales", align_bytes=ALIGN, bufs=bufs)
+            nc.vector.quantize_mx(out=codes[:].bitcast(FP8X4), scales=scales[:], in_=src)
+            return codes, scales
+
+        gathered = held.tile([P, PACK, S], F32, name="gathered")
+        for j in range(PACK):
+            nc.vector.tensor_tensor(gathered[:, j, :], x_sb[j][:].indirect(offsets[:]), gate_sb[:, j, :], MULT)
+
+        x_bf = []
+        for c, engine in enumerate(("vector", "scalar", "vector")):
+            tile = stage.tile([P, CHUNK, PACK], BF16, name="x_bf", align_bytes=ALIGN, bufs=3)
+            copy_on(
+                engine,
+                tile[:].rearrange("p (c i) j -> p c j i", i=4),
+                gathered[:, :, c * CHUNK : (c + 1) * CHUNK].rearrange("p j (c i) -> p c j i", i=4),
+            )
+            x_bf.append(tile)
+        x_q = [quantize(tile[:].rearrange("p s j -> p (s j)"), CHUNK, "x", 3) for tile in x_bf]
+
+        w1_bf = {}
+        w2_bf = {}
+        w2_q = {}
+        h_bf = {}
+        h_q = {}
+        y_sb = {}
+        engines = ("vector", "scalar")
+
+        def cast_w1(e):
+            for g in range(H_PASSES):
+                base = GATE_AT if e == 0 else min(e - 1, E - 3) * W1_SLOT
+                place = base + 4 * KIB * g
+                if e == E - 1:
+                    place = base + 6 * KIB if g == 0 else base + 2 * KIB
+                tile = arena.tile([P, PACK, P, PACK], BF16, name=f"w1_bf{e}_{g}", align_bytes=ALIGN, offset=place)
+                copy_on(
+                    engines[g],
+                    tile[:].rearrange("p t m j -> p m j t"),
+                    w1_raw[e][:, :, g * K_PASS : (g + 1) * K_PASS].rearrange("p j (m t) -> p m j t", t=PACK),
+                )
+                w1_bf[e, g] = tile
+
+        def first_layer(e):
+            x_codes, x_scales = x_q[e // 2]
+            slots = slice((e % 2) * C, (e % 2 + 1) * C)
+            h_bf[e] = stage.tile([P, H_PASSES, C, PACK], BF16, name="h_bf", align_bytes=ALIGN)
+            for g in range(H_PASSES):
+                codes, scales = quantize(w1_bf[e, g][:].rearrange("p t m j -> p (t m j)"), K_PASS, "w1", 4)
+                acc = psum.tile([P, PACK, C], F32, name="acc1", bufs=4)
+                for t in range(PACK):
+                    m_cols = slice(t * P, (t + 1) * P)
+                    nc.tensor.matmul_mx(
+                        out=acc[:, t, :],
+                        lhsT=codes[:, m_cols].bitcast(FP8X4),
+                        lhsT_scale=scales[:, m_cols],
+                        rhs=x_codes[:, slots].bitcast(FP8X4),
+                        rhs_scale=x_scales[:, slots],
+                        start=True,
+                        stop=True,
+                    )
+                nc.scalar.activation(out=h_bf[e][:, g, :, :], in_=acc[:].rearrange("p t c -> p c t"), func=SILU)
+
+        def quantize_h(e):
+            h_q[e] = quantize(h_bf[e][:].rearrange("p g c t -> p (g c t)"), H_PASSES * C, "h", 3)
+
+        def cast_w2(e, g, n0, n1, engine):
+            place = (E - 1) * W1_SLOT + (2 if engine == "vector" else 4) * KIB
+            tile = arena.tile([P, n1 - n0, PACK], BF16, name=f"w2_bf{e}_{g}_{n0}", align_bytes=ALIGN, offset=place)
+            copy_on(
+                engine,
+                tile[:].rearrange("p (c i) j -> p c j i", i=4),
+                w2_raw[e][:, g, :, n0:n1].rearrange("p j (c i) -> p c j i", i=4),
+            )
+            w2_bf[e, g, n0] = tile
+
+        def quantize_w2(e, g, n0, n1):
+            codes, scales = quantize(w2_bf[e, g, n0][:].rearrange("p n j -> p (n j)"), n1 - n0, "w2", 4)
+            for n in range(n0, n1, P):
+                w2_q[e, g, n // P] = (codes[:, n - n0 : n - n0 + P], scales[:, n - n0 : n - n0 + P])
+
+        def second_layer(e, halves):
+            h_codes, h_scales = h_q[e]
+            acc = psum.tile([P, len(halves), C], F32, name="acc2", bufs=2)
+            for place, half in enumerate(halves):
+                for g in range(H_PASSES):
+                    codes, scales = w2_q[e, g, half]
+                    slots = slice(g * C, (g + 1) * C)
+                    nc.tensor.matmul_mx(
+                        out=acc[:, place, :],
+                        lhsT=codes.bitcast(FP8X4),
+                        lhsT_scale=scales,
+                        rhs=h_codes[:, slots].bitcast(FP8X4),
+                        rhs_scale=h_scales[:, slots],
+                        start=(g == 0),
+                        stop=(g == H_PASSES - 1),
+                    )
+            if e // 2 not in y_sb:
+                y_sb[e // 2] = stage.tile([P, N_HALVES, CHUNK], F32, name="y_sb")
+            nc.scalar.copy(
+                out=y_sb[e // 2][:, halves[0] : halves[-1] + 1, (e % 2) * C : (e % 2 + 1) * C], in_=acc[:]
+            )
+
+        def scatter(c, half):
+            chunk_offsets = offsets[:, c * CHUNK // 16 : (c + 1) * CHUNK // 16]
+            nc.vector.tensor_copy(windows[half][:].indirect(chunk_offsets), y_sb[c][:, half, :])
+
+        def whole_w2(e):
+            slot = e if e < E - 2 else E - 1
+            tile = arena.tile(
+                [P, H_PASSES, N, PACK], BF16, name=f"w2_bf{e}", align_bytes=ALIGN, offset=slot * W1_SLOT + 2 * KIB
+            )
+            for engine, g, n0, n1 in (("vector", 0, 0, P), ("scalar", 0, P, N), ("scalar", 1, 0, N)):
+                copy_on(
+                    engine,
+                    tile[:, g, n0:n1, :].rearrange("p (c i) j -> p c j i", i=4),
+                    w2_raw[e][:, g, :, n0:n1].rearrange("p j (c i) -> p c j i", i=4),
+                )
+            w2_bf[e] = tile
+
+        def rest_w2(e):
+            codes, scales = quantize(w2_bf[e][:].rearrange("p g n j -> p (g n j)"), H_PASSES * N, "w2", 4)
+            for g in range(H_PASSES):
+                for half in range(N_HALVES):
+                    m_cols = slice(g * N + half * P, g * N + (half + 1) * P)
+                    w2_q[e, g, half] = (codes[:, m_cols], scales[:, m_cols])
+
+        for e in range(E - 2):
+            cast_w1(e)
+            if e >= 1:
+                quantize_h(e - 1)
+                second_layer(e - 1, (0, 1))
+            first_layer(e)
+            whole_w2(e)
+            if e >= 2:
+                scatter(0, e - 2)
+            rest_w2(e)
+        cast_w1(E - 2)
+        quantize_h(E - 3)
+        second_layer(E - 3, (0, 1))
+        first_layer(E - 2)
+        scatter(1, 0)
+        cast_w1(E - 1)
+        quantize_h(E - 2)
+        first_layer(E - 1)
+        scatter(1, 1)
+        whole_w2(E - 2)
+        rest_w2(E - 2)
+        quantize_h(E - 1)
+        second_layer(E - 2, (0, 1))
+        for g in range(H_PASSES):
+            for half in range(N_HALVES):
+                cast_w2(E - 1, g, half * P, (half + 1) * P, engines[half])
+            for half in range(N_HALVES):
+                quantize_w2(E - 1, g, half * P, (half + 1) * P)
+        for half in range(N_HALVES):
+            second_layer(E - 1, (half,))
+        for half in range(N_HALVES):
+            scatter(E // 2 - 1, half)
+
+        for half in range(N_HALVES):
+            nc.sync.dma_start(out=out[half * P : (half + 1) * P, :], in_=windows[half][:])

@@ -25,19 +25,25 @@ ALIGN = 64
 KIB = 1024
 W1_SLOT = 16 * KIB
 W2_SLOT = 8 * KIB
-GATE_AT = E * W1_SLOT
-W2_AT = GATE_AT + 12 * KIB
-W2_SLOTS = E - 1
+GATE_AT = (E - 1) * W1_SLOT
+GATHERED_AT = GATE_AT + 12 * KIB
+W2_LAST_AT = GATE_AT + W1_SLOT
+W2_AT = W2_LAST_AT + W2_SLOT
+CHUNKS = ((0, 192), (192, 384), (384, 576), (576, 768))
+V_W1 = (160, 160, 160, 160, 192, 96)
+V_W2 = (0, 0, 0, 0, 256)
+X_ENGINES = ("vector", "scalar", "vector")
+Y_AFTER = (2, 3, None, None)
 
 
 def tile_moe_pre_mlp_silu_kernel(tc, xT, w1, w2, gate, offs, out):
     nc = tc.nc
+    last = E - 1
     with ExitStack() as ctx:
         held = ctx.enter_context(tc.tile_pool(name="held", bufs=1))
-        cols = ctx.enter_context(tc.tile_pool(name="cols", bufs=4))
         arena = ctx.enter_context(tc.tile_pool(name="arena", bufs=1))
         stage = ctx.enter_context(tc.tile_pool(name="stage", bufs=2))
-        psum = ctx.enter_context(tc.psum_pool(name="psum", bufs=2))
+        psum = ctx.enter_context(tc.psum_pool(name="psum", bufs=4))
 
         offsets = held.tile([P, S // 16], U16, name="offsets")
         nc.sync.dma_start(offsets[:], offs)
@@ -47,37 +53,35 @@ def tile_moe_pre_mlp_silu_kernel(tc, xT, w1, w2, gate, offs, out):
         x_rows = xT.rearrange("(p j) t -> p j t", j=PACK)
         x_sb = []
         for j in range(PACK):
-            tile = cols.tile([P, T], F32, name="x_sb", tag="cols")
+            tile = held.tile([P, T], F32, name=f"x_sb{j}")
             nc.sync.dma_start(out=tile[:], in_=x_rows[:, j, :])
             x_sb.append(tile)
 
-        w1_raw = {}
-        w2_raw = {}
+        gathered = arena.tile([P, PACK, S], F32, name="gathered", align_bytes=ALIGN, offset=GATHERED_AT)
+        for j in range(PACK):
+            nc.vector.tensor_tensor(gathered[:, j, :], x_sb[j][:].indirect(offsets[:]), gate_sb[:, j, :], MULT)
 
-        def load_w1(e):
+        w1_raw = []
+        w2_raw = []
+        for e in range(E):
             tile = arena.tile([P, PACK, H], F32, name=f"w1_raw{e}", align_bytes=ALIGN, offset=e * W1_SLOT)
-            nc.sync.dma_start(out=tile[:], in_=w1[e].rearrange("(p j) i -> p j i", j=PACK))
-            w1_raw[e] = tile
-
-        def load_w2(e):
-            tile = arena.tile(
-                [P, H_PASSES, PACK, N], F32, name=f"w2_raw{e}", align_bytes=ALIGN, offset=W2_AT + (e % W2_SLOTS) * W2_SLOT
-            )
+            rows = w1[e].rearrange("(p j) i -> p j i", j=PACK)
+            if e < last:
+                nc.sync.dma_start(out=tile[:], in_=rows)
+            else:
+                for g in range(H_PASSES):
+                    cols = slice(g * K_PASS, (g + 1) * K_PASS)
+                    nc.sync.dma_start(out=tile[:, :, cols], in_=rows[:, :, cols])
+            w1_raw.append(tile)
+            place = W2_AT + e * W2_SLOT if e < last else W2_LAST_AT
+            tile = arena.tile([P, H_PASSES, PACK, N], F32, name=f"w2_raw{e}", align_bytes=ALIGN, offset=place)
             rows = w2[e].rearrange("(g p j) n -> p g (j n)", g=H_PASSES, j=PACK)
-            if e < E - 1:
+            if e < last:
                 nc.sync.dma_start(out=tile[:].rearrange("p g j n -> p g (j n)"), in_=rows)
             else:
                 for g in range(H_PASSES):
                     nc.sync.dma_start(out=tile[:, g, :, :].rearrange("p j n -> p (j n)"), in_=rows[:, g, :])
-            w2_raw[e] = tile
-
-        for e in range(E - 2):
-            load_w1(e)
-            load_w2(e)
-        load_w1(E - 2)
-        load_w1(E - 1)
-        load_w2(E - 2)
-        load_w2(E - 1)
+            w2_raw.append(tile)
 
         windows = []
         for half in range(N_HALVES):
@@ -97,12 +101,9 @@ def tile_moe_pre_mlp_silu_kernel(tc, xT, w1, w2, gate, offs, out):
             nc.vector.quantize_mx(out=codes[:].bitcast(FP8X4), scales=scales[:], in_=src)
             return codes, scales
 
-        gathered = held.tile([P, PACK, S], F32, name="gathered")
-        for j in range(PACK):
-            nc.vector.tensor_tensor(gathered[:, j, :], x_sb[j][:].indirect(offsets[:]), gate_sb[:, j, :], MULT)
 
         x_bf = []
-        for c, engine in enumerate(("vector", "scalar", "vector")):
+        for c, engine in enumerate(X_ENGINES):
             tile = stage.tile([P, CHUNK, PACK], BF16, name="x_bf", align_bytes=ALIGN, bufs=3)
             copy_on(
                 engine,
@@ -113,143 +114,146 @@ def tile_moe_pre_mlp_silu_kernel(tc, xT, w1, w2, gate, offs, out):
         x_q = [quantize(tile[:].rearrange("p s j -> p (s j)"), CHUNK, "x", 3) for tile in x_bf]
 
         w1_bf = {}
+        w1_q = {}
         w2_bf = {}
         w2_q = {}
         h_bf = {}
         h_q = {}
+        y_acc = {}
         y_sb = {}
-        engines = ("vector", "scalar")
 
-        def cast_w1(e):
-            for g in range(H_PASSES):
-                base = GATE_AT if e == 0 else min(e - 1, E - 3) * W1_SLOT
-                place = base + 4 * KIB * g
-                if e == E - 1:
-                    place = base + 6 * KIB if g == 0 else base + 2 * KIB
-                tile = arena.tile([P, PACK, P, PACK], BF16, name=f"w1_bf{e}_{g}", align_bytes=ALIGN, offset=place)
-                copy_on(
-                    engines[g],
-                    tile[:].rearrange("p t m j -> p m j t"),
-                    w1_raw[e][:, :, g * K_PASS : (g + 1) * K_PASS].rearrange("p j (m t) -> p m j t", t=PACK),
-                )
-                w1_bf[e, g] = tile
+        def cast_w1(e, g, shares):
+            tile = stage.tile([P, PACK, P, PACK], BF16, name="w1_bf", align_bytes=ALIGN, bufs=3)
+            src = w1_raw[e][:, :, g * K_PASS : (g + 1) * K_PASS].rearrange("p j (m t) -> p m j t", t=PACK)
+            dst = tile[:].rearrange("p t m j -> p m j t")
+            for engine, m0, m1 in shares:
+                if m1 > m0:
+                    copy_on(engine, dst[:, m0:m1, :, :], src[:, m0:m1, :, :])
+            w1_bf[e, g] = tile
 
-        def first_layer(e):
+        def quantize_w1(e, g):
+            w1_q[e, g] = quantize(w1_bf[e, g][:].rearrange("p t m j -> p (t m j)"), K_PASS, "w1", 3)
+
+        def first_layer(e, g):
             x_codes, x_scales = x_q[e // 2]
             slots = slice((e % 2) * C, (e % 2 + 1) * C)
-            h_bf[e] = stage.tile([P, H_PASSES, C, PACK], BF16, name="h_bf", align_bytes=ALIGN)
-            for g in range(H_PASSES):
-                codes, scales = quantize(w1_bf[e, g][:].rearrange("p t m j -> p (t m j)"), K_PASS, "w1", 4)
-                acc = psum.tile([P, PACK, C], F32, name="acc1", bufs=4)
-                for t in range(PACK):
-                    m_cols = slice(t * P, (t + 1) * P)
-                    nc.tensor.matmul_mx(
-                        out=acc[:, t, :],
-                        lhsT=codes[:, m_cols].bitcast(FP8X4),
-                        lhsT_scale=scales[:, m_cols],
-                        rhs=x_codes[:, slots].bitcast(FP8X4),
-                        rhs_scale=x_scales[:, slots],
-                        start=True,
-                        stop=True,
+            codes, scales = w1_q[e, g]
+            acc = psum.tile([P, PACK, C], F32, name="acc1")
+            for t in range(PACK):
+                m_cols = slice(t * P, (t + 1) * P)
+                nc.tensor.matmul_mx(
+                    out=acc[:, t, :],
+                    lhsT=codes[:, m_cols].bitcast(FP8X4),
+                    lhsT_scale=scales[:, m_cols],
+                    rhs=x_codes[:, slots].bitcast(FP8X4),
+                    rhs_scale=x_scales[:, slots],
+                    start=True,
+                    stop=True,
+                )
+            return acc
+
+        def silu(e, g, acc):
+            nc.scalar.activation(out=h_bf[e][:, g, :, :], in_=acc[:].rearrange("p t c -> p c t"), func=SILU)
+
+        def cast_w2(e, tile, shares):
+            for engine, g, n0, n1 in shares:
+                if n1 > n0:
+                    copy_on(
+                        engine,
+                        tile[:, g, n0:n1, :].rearrange("p (c i) j -> p c j i", i=4),
+                        w2_raw[e][:, g, :, n0:n1].rearrange("p j (c i) -> p c j i", i=4),
                     )
-                nc.scalar.activation(out=h_bf[e][:, g, :, :], in_=acc[:].rearrange("p t c -> p c t"), func=SILU)
-
-        def quantize_h(e):
-            h_q[e] = quantize(h_bf[e][:].rearrange("p g c t -> p (g c t)"), H_PASSES * C, "h", 3)
-
-        def cast_w2(e, g, n0, n1, engine):
-            place = (E - 1) * W1_SLOT + (2 if engine == "vector" else 4) * KIB
-            tile = arena.tile([P, n1 - n0, PACK], BF16, name=f"w2_bf{e}_{g}_{n0}", align_bytes=ALIGN, offset=place)
-            copy_on(
-                engine,
-                tile[:].rearrange("p (c i) j -> p c j i", i=4),
-                w2_raw[e][:, g, :, n0:n1].rearrange("p j (c i) -> p c j i", i=4),
-            )
-            w2_bf[e, g, n0] = tile
-
-        def quantize_w2(e, g, n0, n1):
-            codes, scales = quantize(w2_bf[e, g, n0][:].rearrange("p n j -> p (n j)"), n1 - n0, "w2", 4)
-            for n in range(n0, n1, P):
-                w2_q[e, g, n // P] = (codes[:, n - n0 : n - n0 + P], scales[:, n - n0 : n - n0 + P])
 
         def second_layer(e, halves):
-            h_codes, h_scales = h_q[e]
-            acc = psum.tile([P, len(halves), C], F32, name="acc2", bufs=2)
+            acc = psum.tile([P, len(halves), C], F32, name="acc2")
             for place, half in enumerate(halves):
                 for g in range(H_PASSES):
                     codes, scales = w2_q[e, g, half]
-                    slots = slice(g * C, (g + 1) * C)
+                    h_codes, h_scales = h_q[e, g]
                     nc.tensor.matmul_mx(
                         out=acc[:, place, :],
                         lhsT=codes.bitcast(FP8X4),
                         lhsT_scale=scales,
-                        rhs=h_codes[:, slots].bitcast(FP8X4),
-                        rhs_scale=h_scales[:, slots],
+                        rhs=h_codes.bitcast(FP8X4),
+                        rhs_scale=h_scales,
                         start=(g == 0),
                         stop=(g == H_PASSES - 1),
                     )
-            if e // 2 not in y_sb:
-                y_sb[e // 2] = stage.tile([P, N_HALVES, CHUNK], F32, name="y_sb")
+            y_acc[e, halves] = acc
+
+        def leave_psum(c, e, halves):
+            s0, s1 = CHUNKS[c]
+            if c not in y_sb:
+                if Y_AFTER[c] is None:
+                    y_sb[c] = held.tile([P, N_HALVES, s1 - s0], F32, name=f"y_sb{c}")
+                else:
+                    place = Y_AFTER[c] * W1_SLOT
+                    y_sb[c] = arena.tile([P, N_HALVES, s1 - s0], F32, name=f"y_sb{c}", align_bytes=ALIGN, offset=place)
+            lo, hi = max(s0, e * C), min(s1, (e + 1) * C)
             nc.scalar.copy(
-                out=y_sb[e // 2][:, halves[0] : halves[-1] + 1, (e % 2) * C : (e % 2 + 1) * C], in_=acc[:]
+                out=y_sb[c][:, halves[0] : halves[-1] + 1, lo - s0 : hi - s0],
+                in_=y_acc[e, halves][:, :, lo - e * C : hi - e * C],
             )
 
         def scatter(c, half):
-            chunk_offsets = offsets[:, c * CHUNK // 16 : (c + 1) * CHUNK // 16]
-            nc.vector.tensor_copy(windows[half][:].indirect(chunk_offsets), y_sb[c][:, half, :])
+            s0, s1 = CHUNKS[c]
+            nc.vector.tensor_copy(windows[half][:].indirect(offsets[:, s0 // 16 : s1 // 16]), y_sb[c][:, half, :])
 
-        def whole_w2(e):
-            slot = e if e < E - 2 else E - 1
-            tile = arena.tile(
-                [P, H_PASSES, N, PACK], BF16, name=f"w2_bf{e}", align_bytes=ALIGN, offset=slot * W1_SLOT + 2 * KIB
-            )
-            for engine, g, n0, n1 in (("vector", 0, 0, P), ("scalar", 0, P, N), ("scalar", 1, 0, N)):
-                copy_on(
-                    engine,
-                    tile[:, g, n0:n1, :].rearrange("p (c i) j -> p c j i", i=4),
-                    w2_raw[e][:, g, :, n0:n1].rearrange("p j (c i) -> p c j i", i=4),
-                )
-            w2_bf[e] = tile
+        def finish_chunks(e):
+            for c, (s0, s1) in enumerate(CHUNKS):
+                if (s1 - 1) // C == e:
+                    for owner in range(s0 // C, e + 1):
+                        leave_psum(c, owner, (0, 1))
+                    for half in range(N_HALVES):
+                        scatter(c, half)
 
-        def rest_w2(e):
-            codes, scales = quantize(w2_bf[e][:].rearrange("p g n j -> p (g n j)"), H_PASSES * N, "w2", 4)
+        for e in range(last):
+            cast_w1(e, 0, (("vector", 0, min(P, V_W1[e])), ("scalar", min(P, V_W1[e]), P)))
+            cast_w1(e, 1, (("scalar", max(0, V_W1[e] - P), P), ("vector", 0, V_W1[e] - P)))
+            accs = []
+            for g in range(H_PASSES):
+                quantize_w1(e, g)
+                accs.append(first_layer(e, g))
+            if e >= 1:
+                finish_chunks(e - 1)
+            tile = stage.tile([P, H_PASSES, N, PACK], BF16, name="w2_bf", align_bytes=ALIGN)
+            cast_w2(e, tile, (("vector", 0, 0, V_W2[e]), ("scalar", 0, V_W2[e], N), ("scalar", 1, 0, N)))
+            place = W2_AT + e * W2_SLOT
+            h_bf[e] = arena.tile([P, H_PASSES, C, PACK], BF16, name=f"h_bf{e}", align_bytes=ALIGN, offset=place)
+            for g in range(H_PASSES):
+                silu(e, g, accs[g])
+            codes, scales = quantize(tile[:].rearrange("p g n j -> p (g n j)"), H_PASSES * N, "w2", 2)
             for g in range(H_PASSES):
                 for half in range(N_HALVES):
                     m_cols = slice(g * N + half * P, g * N + (half + 1) * P)
                     w2_q[e, g, half] = (codes[:, m_cols], scales[:, m_cols])
+            codes, scales = quantize(h_bf[e][:].rearrange("p g c t -> p (g c t)"), H_PASSES * C, "h", 2)
+            for g in range(H_PASSES):
+                h_q[e, g] = (codes[:, g * C : (g + 1) * C], scales[:, g * C : (g + 1) * C])
+            second_layer(e, (0, 1))
 
-        for e in range(E - 2):
-            cast_w1(e)
-            if e >= 1:
-                quantize_h(e - 1)
-                second_layer(e - 1, (0, 1))
-            first_layer(e)
-            whole_w2(e)
-            if e >= 2:
-                scatter(0, e - 2)
-            rest_w2(e)
-        cast_w1(E - 2)
-        quantize_h(E - 3)
-        second_layer(E - 3, (0, 1))
-        first_layer(E - 2)
-        scatter(1, 0)
-        cast_w1(E - 1)
-        quantize_h(E - 2)
-        first_layer(E - 1)
-        scatter(1, 1)
-        whole_w2(E - 2)
-        rest_w2(E - 2)
-        quantize_h(E - 1)
-        second_layer(E - 2, (0, 1))
+        h_bf[last] = held.tile([P, H_PASSES, C, PACK], BF16, name="h_last", align_bytes=ALIGN)
+        share = V_W1[last] // 2
         for g in range(H_PASSES):
+            cast_w1(last, g, (("vector", 0, share), ("scalar", share, P)))
+            quantize_w1(last, g)
+            silu(last, g, first_layer(last, g))
+            codes, scales = quantize(h_bf[last][:, g, :, :].rearrange("p c t -> p (c t)"), C, "h_last", 2)
+            h_q[last, g] = (codes[:], scales[:])
+            if g == 0:
+                finish_chunks(last - 1)
+        final = len(CHUNKS) - 1
+        leave_psum(final, last - 1, (0, 1))
+        tile = stage.tile([P, H_PASSES, N, PACK], BF16, name="w2_bf", align_bytes=ALIGN)
+        for g in range(H_PASSES):
+            cast_w2(last, tile, (("vector", g, 0, P), ("scalar", g, P, N)))
             for half in range(N_HALVES):
-                cast_w2(E - 1, g, half * P, (half + 1) * P, engines[half])
-            for half in range(N_HALVES):
-                quantize_w2(E - 1, g, half * P, (half + 1) * P)
+                cols = slice(half * P, (half + 1) * P)
+                codes, scales = quantize(tile[:, g, cols, :].rearrange("p n j -> p (n j)"), P, "w2_last", 4)
+                w2_q[last, g, half] = (codes[:], scales[:])
         for half in range(N_HALVES):
-            second_layer(E - 1, (half,))
+            second_layer(last, (half,))
+            leave_psum(final, last, (half,))
         for half in range(N_HALVES):
-            scatter(E // 2 - 1, half)
-
-        for half in range(N_HALVES):
+            scatter(final, half)
             nc.sync.dma_start(out=out[half * P : (half + 1) * P, :], in_=windows[half][:])

@@ -27,13 +27,14 @@ W1_SLOT = 16 * KIB
 W2_SLOT = 8 * KIB
 GATE_AT = (E - 1) * W1_SLOT
 GATHERED_AT = GATE_AT + 12 * KIB
-W2_LAST_AT = GATE_AT + W1_SLOT
-W2_AT = W2_LAST_AT + W2_SLOT
+W1_LAST_AT = (GATE_AT, GATE_AT + 8 * KIB)
+W2_LAST_AT = (GATE_AT + 16 * KIB, GATE_AT + 20 * KIB)
+W2_AT = GATE_AT + 24 * KIB
 CHUNKS = ((0, 192), (192, 384), (384, 576), (576, 768))
-V_W1 = (160, 160, 160, 160, 192, 96)
-V_W2 = (0, 0, 0, 0, 256)
+V_W1 = (160, 160, 160, 160, 144)
+V_W1_LAST = (96, 64)
+V_W2 = (0, 0, 0, 0, 192)
 X_ENGINES = ("vector", "scalar", "vector")
-Y_AFTER = (2, 3, None, None)
 
 
 def tile_moe_pre_mlp_silu_kernel(tc, xT, w1, w2, gate, offs, out):
@@ -45,11 +46,13 @@ def tile_moe_pre_mlp_silu_kernel(tc, xT, w1, w2, gate, offs, out):
         stage = ctx.enter_context(tc.tile_pool(name="stage", bufs=2))
         psum = ctx.enter_context(tc.psum_pool(name="psum", bufs=4))
 
-        offsets = held.tile([P, S // 16], U16, name="offsets")
-        nc.sync.dma_start(offsets[:], offs)
+        def placed(shape, dtype, name, place):
+            return arena.tile(shape, dtype, name=name, align_bytes=ALIGN, offset=place)
 
+        offsets = held.tile([P, S // 16], U16, name="offsets")
         gate_sb = arena.tile([P, PACK, S], F32, name="gate_sb", align_bytes=ALIGN, offset=GATE_AT)
         nc.sync.dma_start(out=gate_sb[:], in_=gate.rearrange("(p j) s -> p j s", j=PACK))
+        nc.sync.dma_start(offsets[:], offs)
         x_rows = xT.rearrange("(p j) t -> p j t", j=PACK)
         x_sb = []
         for j in range(PACK):
@@ -61,27 +64,29 @@ def tile_moe_pre_mlp_silu_kernel(tc, xT, w1, w2, gate, offs, out):
         for j in range(PACK):
             nc.vector.tensor_tensor(gathered[:, j, :], x_sb[j][:].indirect(offsets[:]), gate_sb[:, j, :], MULT)
 
-        w1_raw = []
-        w2_raw = []
+        w1_raw = {}
+        w2_raw = {}
         for e in range(E):
-            tile = arena.tile([P, PACK, H], F32, name=f"w1_raw{e}", align_bytes=ALIGN, offset=e * W1_SLOT)
-            rows = w1[e].rearrange("(p j) i -> p j i", j=PACK)
+            w1_rows = w1[e].rearrange("(p j) i -> p j i", j=PACK)
+            w2_rows = w2[e].rearrange("(g p j) n -> p g (j n)", g=H_PASSES, j=PACK)
             if e < last:
-                nc.sync.dma_start(out=tile[:], in_=rows)
+                tile = placed([P, PACK, H], F32, f"w1_raw{e}", e * W1_SLOT)
+                nc.sync.dma_start(out=tile[:], in_=w1_rows)
+                for g in range(H_PASSES):
+                    w1_raw[e, g] = tile[:, :, g * K_PASS : (g + 1) * K_PASS]
+                tile = placed([P, H_PASSES, PACK, N], F32, f"w2_raw{e}", W2_AT + e * W2_SLOT)
+                nc.sync.dma_start(out=tile[:].rearrange("p g j n -> p g (j n)"), in_=w2_rows)
+                for g in range(H_PASSES):
+                    w2_raw[e, g] = tile[:, g, :, :]
             else:
                 for g in range(H_PASSES):
-                    cols = slice(g * K_PASS, (g + 1) * K_PASS)
-                    nc.sync.dma_start(out=tile[:, :, cols], in_=rows[:, :, cols])
-            w1_raw.append(tile)
-            place = W2_AT + e * W2_SLOT if e < last else W2_LAST_AT
-            tile = arena.tile([P, H_PASSES, PACK, N], F32, name=f"w2_raw{e}", align_bytes=ALIGN, offset=place)
-            rows = w2[e].rearrange("(g p j) n -> p g (j n)", g=H_PASSES, j=PACK)
-            if e < last:
-                nc.sync.dma_start(out=tile[:].rearrange("p g j n -> p g (j n)"), in_=rows)
-            else:
+                    tile = placed([P, PACK, K_PASS], F32, f"w1_raw{e}_{g}", W1_LAST_AT[g])
+                    nc.sync.dma_start(out=tile[:], in_=w1_rows[:, :, g * K_PASS : (g + 1) * K_PASS])
+                    w1_raw[e, g] = tile[:]
                 for g in range(H_PASSES):
-                    nc.sync.dma_start(out=tile[:, g, :, :].rearrange("p j n -> p (j n)"), in_=rows[:, g, :])
-            w2_raw.append(tile)
+                    tile = placed([P, PACK, N], F32, f"w2_raw{e}_{g}", W2_LAST_AT[g])
+                    nc.sync.dma_start(out=tile[:].rearrange("p j n -> p (j n)"), in_=w2_rows[:, g, :])
+                    w2_raw[e, g] = tile[:]
 
         windows = []
         for half in range(N_HALVES):
@@ -95,8 +100,11 @@ def tile_moe_pre_mlp_silu_kernel(tc, xT, w1, w2, gate, offs, out):
             else:
                 nc.scalar.copy(out=dst, in_=src)
 
-        def quantize(src, words, name, bufs):
-            codes = stage.tile([P, words], U32, name=name + "_codes", align_bytes=ALIGN, bufs=bufs)
+        def quantize(src, words, name, bufs, place=None):
+            if place is None:
+                codes = stage.tile([P, words], U32, name=name + "_codes", align_bytes=ALIGN, bufs=bufs)
+            else:
+                codes = placed([P, words], U32, name + "_placed_codes", place)
             scales = stage.tile([P, words], U8, name=name + "_scales", align_bytes=ALIGN, bufs=bufs)
             nc.vector.quantize_mx(out=codes[:].bitcast(FP8X4), scales=scales[:], in_=src)
             return codes, scales
@@ -124,7 +132,7 @@ def tile_moe_pre_mlp_silu_kernel(tc, xT, w1, w2, gate, offs, out):
 
         def cast_w1(e, g, shares):
             tile = stage.tile([P, PACK, P, PACK], BF16, name="w1_bf", align_bytes=ALIGN, bufs=3)
-            src = w1_raw[e][:, :, g * K_PASS : (g + 1) * K_PASS].rearrange("p j (m t) -> p m j t", t=PACK)
+            src = w1_raw[e, g].rearrange("p j (m t) -> p m j t", t=PACK)
             dst = tile[:].rearrange("p t m j -> p m j t")
             for engine, m0, m1 in shares:
                 if m1 > m0:
@@ -152,8 +160,8 @@ def tile_moe_pre_mlp_silu_kernel(tc, xT, w1, w2, gate, offs, out):
                 )
             return acc
 
-        def silu(e, g, acc):
-            nc.scalar.activation(out=h_bf[e][:, g, :, :], in_=acc[:].rearrange("p t c -> p c t"), func=SILU)
+        def silu(dst, acc):
+            nc.scalar.activation(out=dst, in_=acc[:].rearrange("p t c -> p c t"), func=SILU)
 
         def cast_w2(e, tile, shares):
             for engine, g, n0, n1 in shares:
@@ -161,7 +169,7 @@ def tile_moe_pre_mlp_silu_kernel(tc, xT, w1, w2, gate, offs, out):
                     copy_on(
                         engine,
                         tile[:, g, n0:n1, :].rearrange("p (c i) j -> p c j i", i=4),
-                        w2_raw[e][:, g, :, n0:n1].rearrange("p j (c i) -> p c j i", i=4),
+                        w2_raw[e, g][:, :, n0:n1].rearrange("p j (c i) -> p c j i", i=4),
                     )
 
         def second_layer(e, halves):
@@ -181,79 +189,99 @@ def tile_moe_pre_mlp_silu_kernel(tc, xT, w1, w2, gate, offs, out):
                     )
             y_acc[e, halves] = acc
 
-        def leave_psum(c, e, halves):
+        def leave_psum(c, e, halves, source):
             s0, s1 = CHUNKS[c]
-            if c not in y_sb:
-                if Y_AFTER[c] is None:
-                    y_sb[c] = held.tile([P, N_HALVES, s1 - s0], F32, name=f"y_sb{c}")
-                else:
-                    place = Y_AFTER[c] * W1_SLOT
-                    y_sb[c] = arena.tile([P, N_HALVES, s1 - s0], F32, name=f"y_sb{c}", align_bytes=ALIGN, offset=place)
             lo, hi = max(s0, e * C), min(s1, (e + 1) * C)
+            first = halves[0] - source[0]
+            tile, base = y_sb[c, halves[0]]
             nc.scalar.copy(
-                out=y_sb[c][:, halves[0] : halves[-1] + 1, lo - s0 : hi - s0],
-                in_=y_acc[e, halves][:, :, lo - e * C : hi - e * C],
+                out=tile[:, halves[0] - base : halves[-1] + 1 - base, lo - s0 : hi - s0],
+                in_=y_acc[e, source][:, first : first + len(halves), lo - e * C : hi - e * C],
             )
 
         def scatter(c, half):
             s0, s1 = CHUNKS[c]
-            nc.vector.tensor_copy(windows[half][:].indirect(offsets[:, s0 // 16 : s1 // 16]), y_sb[c][:, half, :])
+            tile, base = y_sb[c, half]
+            nc.vector.tensor_copy(windows[half][:].indirect(offsets[:, s0 // 16 : s1 // 16]), tile[:, half - base, :])
 
-        def finish_chunks(e):
-            for c, (s0, s1) in enumerate(CHUNKS):
-                if (s1 - 1) // C == e:
-                    for owner in range(s0 // C, e + 1):
-                        leave_psum(c, owner, (0, 1))
-                    for half in range(N_HALVES):
-                        scatter(c, half)
+        def y_tile(c, halves, place):
+            s0, s1 = CHUNKS[c]
+            tile = placed([P, len(halves), s1 - s0], F32, f"y_sb{c}_{halves[0]}", place)
+            for half in halves:
+                y_sb[c, half] = (tile, halves[0])
+
+        def finish_chunk(c, halves, place):
+            s0, s1 = CHUNKS[c]
+            y_tile(c, halves, place)
+            for owner in range(s0 // C, (s1 - 1) // C + 1):
+                leave_psum(c, owner, halves, (0, 1))
+
+        def quantize_h(e, place):
+            codes, scales = quantize(h_bf[e][:].rearrange("p g c t -> p (g c t)"), H_PASSES * C, "h", 2, place)
+            for g in range(H_PASSES):
+                h_q[e, g] = (codes[:, g * C : (g + 1) * C], scales[:, g * C : (g + 1) * C])
+            second_layer(e, (0, 1))
 
         for e in range(last):
-            cast_w1(e, 0, (("vector", 0, min(P, V_W1[e])), ("scalar", min(P, V_W1[e]), P)))
-            cast_w1(e, 1, (("scalar", max(0, V_W1[e] - P), P), ("vector", 0, V_W1[e] - P)))
+            cast_w1(e, 0, (("vector", 0, P),))
+            cast_w1(e, 1, (("scalar", V_W1[e] - P, P), ("vector", 0, V_W1[e] - P)))
             accs = []
             for g in range(H_PASSES):
                 quantize_w1(e, g)
                 accs.append(first_layer(e, g))
-            if e >= 1:
-                finish_chunks(e - 1)
+            if e in (2, 3):
+                finish_chunk(e - 2, (0, 1), e * W1_SLOT)
+                for half in range(N_HALVES):
+                    scatter(e - 2, half)
             tile = stage.tile([P, H_PASSES, N, PACK], BF16, name="w2_bf", align_bytes=ALIGN)
             cast_w2(e, tile, (("vector", 0, 0, V_W2[e]), ("scalar", 0, V_W2[e], N), ("scalar", 1, 0, N)))
-            place = W2_AT + e * W2_SLOT
-            h_bf[e] = arena.tile([P, H_PASSES, C, PACK], BF16, name=f"h_bf{e}", align_bytes=ALIGN, offset=place)
+            h_bf[e] = placed([P, H_PASSES, C, PACK], BF16, f"h_bf{e}", W2_AT + e * W2_SLOT)
             for g in range(H_PASSES):
-                silu(e, g, accs[g])
+                silu(h_bf[e][:, g, :, :], accs[g])
             codes, scales = quantize(tile[:].rearrange("p g n j -> p (g n j)"), H_PASSES * N, "w2", 2)
             for g in range(H_PASSES):
                 for half in range(N_HALVES):
                     m_cols = slice(g * N + half * P, g * N + (half + 1) * P)
                     w2_q[e, g, half] = (codes[:, m_cols], scales[:, m_cols])
-            codes, scales = quantize(h_bf[e][:].rearrange("p g c t -> p (g c t)"), H_PASSES * C, "h", 2)
-            for g in range(H_PASSES):
-                h_q[e, g] = (codes[:, g * C : (g + 1) * C], scales[:, g * C : (g + 1) * C])
-            second_layer(e, (0, 1))
+            if e < last - 1:
+                quantize_h(e, None)
 
-        h_bf[last] = held.tile([P, H_PASSES, C, PACK], BF16, name="h_last", align_bytes=ALIGN)
-        share = V_W1[last] // 2
-        for g in range(H_PASSES):
-            cast_w1(last, g, (("vector", 0, share), ("scalar", share, P)))
-            quantize_w1(last, g)
-            silu(last, g, first_layer(last, g))
-            codes, scales = quantize(h_bf[last][:, g, :, :].rearrange("p c t -> p (c t)"), C, "h_last", 2)
+        def quantize_h_last(g, h_tile):
+            codes, scales = quantize(h_tile[:].rearrange("p c t -> p (c t)"), C, "h_last", 2)
             h_q[last, g] = (codes[:], scales[:])
-            if g == 0:
-                finish_chunks(last - 1)
-        final = len(CHUNKS) - 1
-        leave_psum(final, last - 1, (0, 1))
+
+        cast_w1(last, 0, (("vector", 0, V_W1_LAST[0]), ("scalar", V_W1_LAST[0], P)))
+        quantize_h(last - 1, W1_LAST_AT[0])
+        quantize_w1(last, 0)
+        acc0 = first_layer(last, 0)
+        cast_w1(last, 1, (("vector", 0, V_W1_LAST[1]), ("scalar", V_W1_LAST[1], P)))
+        quantize_w1(last, 1)
+        acc1 = first_layer(last, 1)
+        finish_chunk(2, (0,), W1_LAST_AT[1])
+        h0 = placed([P, C, PACK], BF16, "h_last0", W1_LAST_AT[1] + KIB)
+        silu(h0[:], acc0)
+        scatter(2, 0)
+        quantize_h_last(0, h0)
         tile = stage.tile([P, H_PASSES, N, PACK], BF16, name="w2_bf", align_bytes=ALIGN)
-        for g in range(H_PASSES):
-            cast_w2(last, tile, (("vector", g, 0, P), ("scalar", g, P, N)))
-            for half in range(N_HALVES):
-                cols = slice(half * P, (half + 1) * P)
-                codes, scales = quantize(tile[:, g, cols, :].rearrange("p n j -> p (n j)"), P, "w2_last", 4)
-                w2_q[last, g, half] = (codes[:], scales[:])
+        cast_w2(last, tile, (("scalar", 0, 0, N),))
+        h1 = placed([P, C, PACK], BF16, "h_last1", W2_LAST_AT[0])
+        silu(h1[:], acc1)
+        cast_w2(last, tile, (("vector", 1, 0, P), ("scalar", 1, P, N)))
+        codes, scales = quantize(tile[:, 0, :, :].rearrange("p n j -> p (n j)"), N, "w2_last", 3)
+        for half in range(N_HALVES):
+            w2_q[last, 0, half] = (codes[:, half * P : (half + 1) * P], scales[:, half * P : (half + 1) * P])
+        quantize_h_last(1, h1)
+        for half in range(N_HALVES):
+            cols = slice(half * P, (half + 1) * P)
+            codes, scales = quantize(tile[:, 1, cols, :].rearrange("p n j -> p (n j)"), P, "w2_last", 3)
+            w2_q[last, 1, half] = (codes[:], scales[:])
+        finish_chunk(2, (1,), W2_LAST_AT[1])
+        y_tile(3, (0, 1), W2_LAST_AT[0] + KIB)
+        leave_psum(3, last - 1, (0, 1), (0, 1))
+        scatter(2, 1)
         for half in range(N_HALVES):
             second_layer(last, (half,))
-            leave_psum(final, last, (half,))
+            leave_psum(3, last, (half,), (half,))
         for half in range(N_HALVES):
-            scatter(final, half)
+            scatter(3, half)
             nc.sync.dma_start(out=out[half * P : (half + 1) * P, :], in_=windows[half][:])

@@ -31,9 +31,17 @@ W1_LAST_AT = (GATE_AT, GATE_AT + 8 * KIB)
 W2_LAST_AT = (GATE_AT + 16 * KIB, GATE_AT + 20 * KIB)
 W2_AT = GATE_AT + 24 * KIB
 CHUNKS = ((0, 192), (192, 384), (384, 576), (576, 768))
-V_W1 = (160, 160, 160, 160, 144)
-V_W1_LAST = (96, 64)
-V_W2 = (0, 0, 0, 0, 192)
+V_W1 = (160, 160, 176, 160, 192)
+V_W1_LAST = (112, 48)
+DELAY_11 = 0
+Y21_AT = 1
+V_B51 = 1
+V_B50 = 1
+H1_AT = 1
+H4_AT = 1
+QH4_AT = 1
+V_B511 = 0
+V_W2 = (0, 128, 0, 0, 64)
 X_ENGINES = ("vector", "scalar", "vector")
 
 
@@ -115,8 +123,8 @@ def tile_moe_pre_mlp_silu_kernel(tc, xT, w1, w2, gate, offs, out):
             tile = stage.tile([P, CHUNK, PACK], BF16, name="x_bf", align_bytes=ALIGN, bufs=3)
             copy_on(
                 engine,
-                tile[:].rearrange("p (c i) j -> p c j i", i=4),
-                gathered[:, :, c * CHUNK : (c + 1) * CHUNK].rearrange("p j (c i) -> p c j i", i=4),
+                tile[:].rearrange("p (c i) j -> p c j i", i=2),
+                gathered[:, :, c * CHUNK : (c + 1) * CHUNK].rearrange("p j (c i) -> p c j i", i=2),
             )
             x_bf.append(tile)
         x_q = [quantize(tile[:].rearrange("p s j -> p (s j)"), CHUNK, "x", 3) for tile in x_bf]
@@ -168,8 +176,8 @@ def tile_moe_pre_mlp_silu_kernel(tc, xT, w1, w2, gate, offs, out):
                 if n1 > n0:
                     copy_on(
                         engine,
-                        tile[:, g, n0:n1, :].rearrange("p (c i) j -> p c j i", i=4),
-                        w2_raw[e, g][:, :, n0:n1].rearrange("p j (c i) -> p c j i", i=4),
+                        tile[:, g, n0:n1, :].rearrange("p (c i) j -> p c j i", i=2),
+                        w2_raw[e, g][:, :, n0:n1].rearrange("p j (c i) -> p c j i", i=2),
                     )
 
         def second_layer(e, halves):
@@ -229,13 +237,16 @@ def tile_moe_pre_mlp_silu_kernel(tc, xT, w1, w2, gate, offs, out):
             for g in range(H_PASSES):
                 quantize_w1(e, g)
                 accs.append(first_layer(e, g))
-            if e in (2, 3):
+            if e == 2 or (e == 3 and not DELAY_11):
                 finish_chunk(e - 2, (0, 1), e * W1_SLOT)
                 for half in range(N_HALVES):
                     scatter(e - 2, half)
+            elif e >= 3 and DELAY_11:
+                finish_chunk(1, (e - 3,), e * W1_SLOT)
+                scatter(1, e - 3)
             tile = stage.tile([P, H_PASSES, N, PACK], BF16, name="w2_bf", align_bytes=ALIGN)
             cast_w2(e, tile, (("vector", 0, 0, V_W2[e]), ("scalar", 0, V_W2[e], N), ("scalar", 1, 0, N)))
-            h_bf[e] = placed([P, H_PASSES, C, PACK], BF16, f"h_bf{e}", W2_AT + e * W2_SLOT)
+            h_bf[e] = placed([P, H_PASSES, C, PACK], BF16, f"h_bf{e}", W2_AT + e * W2_SLOT if e < last - 1 or H4_AT else e * W1_SLOT)
             for g in range(H_PASSES):
                 silu(h_bf[e][:, g, :, :], accs[g])
             codes, scales = quantize(tile[:].rearrange("p g n j -> p (g n j)"), H_PASSES * N, "w2", 2)
@@ -251,7 +262,7 @@ def tile_moe_pre_mlp_silu_kernel(tc, xT, w1, w2, gate, offs, out):
             h_q[last, g] = (codes[:], scales[:])
 
         cast_w1(last, 0, (("vector", 0, V_W1_LAST[0]), ("scalar", V_W1_LAST[0], P)))
-        quantize_h(last - 1, W1_LAST_AT[0])
+        quantize_h(last - 1, W1_LAST_AT[0] if QH4_AT else None)
         quantize_w1(last, 0)
         acc0 = first_layer(last, 0)
         cast_w1(last, 1, (("vector", 0, V_W1_LAST[1]), ("scalar", V_W1_LAST[1], P)))
@@ -262,26 +273,40 @@ def tile_moe_pre_mlp_silu_kernel(tc, xT, w1, w2, gate, offs, out):
         silu(h0[:], acc0)
         scatter(2, 0)
         quantize_h_last(0, h0)
-        tile = stage.tile([P, H_PASSES, N, PACK], BF16, name="w2_bf", align_bytes=ALIGN)
-        cast_w2(last, tile, (("scalar", 0, 0, N),))
-        h1 = placed([P, C, PACK], BF16, "h_last1", W2_LAST_AT[0])
+        halves_bf = [stage.tile([P, H_PASSES, P, PACK], BF16, name="w2_last_bf", align_bytes=ALIGN) for half in range(N_HALVES)]
+
+        def cast_last(engine, g, half):
+            copy_on(
+                engine,
+                halves_bf[half][:, g, :, :].rearrange("p (c i) j -> p c j i", i=2),
+                w2_raw[last, g][:, :, half * P : (half + 1) * P].rearrange("p j (c i) -> p c j i", i=2),
+            )
+
+        def quantize_last(half):
+            codes, scales = quantize(halves_bf[half][:].rearrange("p g n j -> p (g n j)"), N, "w2_last", 2)
+            for g in range(H_PASSES):
+                w2_q[last, g, half] = (codes[:, g * P : (g + 1) * P], scales[:, g * P : (g + 1) * P])
+
+        cast_last("vector" if V_B50 else "scalar", 0, 0)
+        cast_last("scalar", 0, 1)
+        h1 = placed([P, C, PACK], BF16, "h_last1", W2_LAST_AT[0] if H1_AT == 0 else W1_LAST_AT[1] + 2 * KIB)
         silu(h1[:], acc1)
-        cast_w2(last, tile, (("vector", 1, 0, P), ("scalar", 1, P, N)))
-        codes, scales = quantize(tile[:, 0, :, :].rearrange("p n j -> p (n j)"), N, "w2_last", 3)
-        for half in range(N_HALVES):
-            w2_q[last, 0, half] = (codes[:, half * P : (half + 1) * P], scales[:, half * P : (half + 1) * P])
+        if Y21_AT == 0:
+            finish_chunk(2, (1,), W2_LAST_AT[0] + 3 * KIB)
+        cast_last("vector" if V_B51 else "scalar", 1, 0)
+        cast_last("vector" if V_B511 else "scalar", 1, 1)
         quantize_h_last(1, h1)
-        for half in range(N_HALVES):
-            cols = slice(half * P, (half + 1) * P)
-            codes, scales = quantize(tile[:, 1, cols, :].rearrange("p n j -> p (n j)"), P, "w2_last", 3)
-            w2_q[last, 1, half] = (codes[:], scales[:])
-        finish_chunk(2, (1,), W2_LAST_AT[1])
-        y_tile(3, (0, 1), W2_LAST_AT[0] + KIB)
+        quantize_last(0)
+        if Y21_AT == 1:
+            finish_chunk(2, (1,), W2_LAST_AT[1])
+        y_tile(3, (0, 1), W2_LAST_AT[1] + KIB)
         leave_psum(3, last - 1, (0, 1), (0, 1))
+        second_layer(last, (0,))
+        leave_psum(3, last, (0,), (0,))
+        quantize_last(1)
         scatter(2, 1)
-        for half in range(N_HALVES):
-            second_layer(last, (half,))
-            leave_psum(3, last, (half,), (half,))
+        second_layer(last, (1,))
+        leave_psum(3, last, (1,), (1,))
         for half in range(N_HALVES):
             scatter(3, half)
             nc.sync.dma_start(out=out[half * P : (half + 1) * P, :], in_=windows[half][:])

@@ -20,34 +20,33 @@ PACK = 4
 K_PASS = P * PACK
 H_PASSES = H // K_PASS
 N_HALVES = N // P
-CHUNK = 2 * C
+BOTH = (0, 1)
+LAST = E - 1
+LIST_COLUMN = 16
 ALIGN = 64
+RUN = 2
+
+X_SLOTS = 2 * C
+X_ENGINES = ("vector", "scalar", "vector")
+
+PIECE = T // 8
+
+V_W1 = (32, 32, 48, 32, 64)
+V_W2 = (0, 128, 0, 0, 64)
+V_W1_LAST = (112, 48)
+
 KIB = 1024
-W1_SLOT = 16 * KIB
-W2_SLOT = 8 * KIB
-GATE_AT = (E - 1) * W1_SLOT
+W1_BYTES = 16 * KIB
+W2_BYTES = 8 * KIB
+GATE_AT = LAST * W1_BYTES
 GATHERED_AT = GATE_AT + 12 * KIB
 W1_LAST_AT = (GATE_AT, GATE_AT + 8 * KIB)
 W2_LAST_AT = (GATE_AT + 16 * KIB, GATE_AT + 20 * KIB)
 W2_AT = GATE_AT + 24 * KIB
-CHUNKS = ((0, 192), (192, 384), (384, 576), (576, 768))
-V_W1 = (160, 160, 176, 160, 192)
-V_W1_LAST = (112, 48)
-DELAY_11 = 0
-Y21_AT = 1
-V_B51 = 1
-V_B50 = 1
-H1_AT = 1
-H4_AT = 1
-QH4_AT = 1
-V_B511 = 0
-V_W2 = (0, 128, 0, 0, 64)
-X_ENGINES = ("vector", "scalar", "vector")
 
 
 def tile_moe_pre_mlp_silu_kernel(tc, xT, w1, w2, gate, offs, out):
     nc = tc.nc
-    last = E - 1
     with ExitStack() as ctx:
         held = ctx.enter_context(tc.tile_pool(name="held", bufs=1))
         arena = ctx.enter_context(tc.tile_pool(name="arena", bufs=1))
@@ -57,18 +56,18 @@ def tile_moe_pre_mlp_silu_kernel(tc, xT, w1, w2, gate, offs, out):
         def placed(shape, dtype, name, place):
             return arena.tile(shape, dtype, name=name, align_bytes=ALIGN, offset=place)
 
-        offsets = held.tile([P, S // 16], U16, name="offsets")
-        gate_sb = arena.tile([P, PACK, S], F32, name="gate_sb", align_bytes=ALIGN, offset=GATE_AT)
+        offsets = held.tile([P, S // LIST_COLUMN], U16, name="offsets")
+        gate_sb = placed([P, PACK, S], F32, "gate_sb", GATE_AT)
         nc.sync.dma_start(out=gate_sb[:], in_=gate.rearrange("(p j) s -> p j s", j=PACK))
         nc.sync.dma_start(offsets[:], offs)
         x_rows = xT.rearrange("(p j) t -> p j t", j=PACK)
         x_sb = []
         for j in range(PACK):
-            tile = held.tile([P, T], F32, name=f"x_sb{j}")
-            nc.sync.dma_start(out=tile[:], in_=x_rows[:, j, :])
-            x_sb.append(tile)
+            x_tile = held.tile([P, T], F32, name=f"x_sb{j}")
+            nc.sync.dma_start(out=x_tile[:], in_=x_rows[:, j, :])
+            x_sb.append(x_tile)
 
-        gathered = arena.tile([P, PACK, S], F32, name="gathered", align_bytes=ALIGN, offset=GATHERED_AT)
+        gathered = placed([P, PACK, S], F32, "gathered", GATHERED_AT)
         for j in range(PACK):
             nc.vector.tensor_tensor(gathered[:, j, :], x_sb[j][:].indirect(offsets[:]), gate_sb[:, j, :], MULT)
 
@@ -77,36 +76,43 @@ def tile_moe_pre_mlp_silu_kernel(tc, xT, w1, w2, gate, offs, out):
         for e in range(E):
             w1_rows = w1[e].rearrange("(p j) i -> p j i", j=PACK)
             w2_rows = w2[e].rearrange("(g p j) n -> p g (j n)", g=H_PASSES, j=PACK)
-            if e < last:
-                tile = placed([P, PACK, H], F32, f"w1_raw{e}", e * W1_SLOT)
-                nc.sync.dma_start(out=tile[:], in_=w1_rows)
+            if e < LAST:
+                raw = placed([P, PACK, H], F32, f"w1_raw{e}", e * W1_BYTES)
+                nc.sync.dma_start(out=raw[:], in_=w1_rows)
                 for g in range(H_PASSES):
-                    w1_raw[e, g] = tile[:, :, g * K_PASS : (g + 1) * K_PASS]
-                tile = placed([P, H_PASSES, PACK, N], F32, f"w2_raw{e}", W2_AT + e * W2_SLOT)
-                nc.sync.dma_start(out=tile[:].rearrange("p g j n -> p g (j n)"), in_=w2_rows)
+                    w1_raw[e, g] = raw[:, :, g * K_PASS : (g + 1) * K_PASS]
+                raw = placed([P, H_PASSES, PACK, N], F32, f"w2_raw{e}", W2_AT + e * W2_BYTES)
+                nc.sync.dma_start(out=raw[:].rearrange("p g j n -> p g (j n)"), in_=w2_rows)
                 for g in range(H_PASSES):
-                    w2_raw[e, g] = tile[:, g, :, :]
+                    w2_raw[e, g] = raw[:, g, :, :]
             else:
                 for g in range(H_PASSES):
-                    tile = placed([P, PACK, K_PASS], F32, f"w1_raw{e}_{g}", W1_LAST_AT[g])
-                    nc.sync.dma_start(out=tile[:], in_=w1_rows[:, :, g * K_PASS : (g + 1) * K_PASS])
-                    w1_raw[e, g] = tile[:]
+                    raw = placed([P, PACK, K_PASS], F32, f"w1_raw{e}_{g}", W1_LAST_AT[g])
+                    nc.sync.dma_start(out=raw[:], in_=w1_rows[:, :, g * K_PASS : (g + 1) * K_PASS])
+                    w1_raw[e, g] = raw[:]
                 for g in range(H_PASSES):
-                    tile = placed([P, PACK, N], F32, f"w2_raw{e}_{g}", W2_LAST_AT[g])
-                    nc.sync.dma_start(out=tile[:].rearrange("p j n -> p (j n)"), in_=w2_rows[:, g, :])
-                    w2_raw[e, g] = tile[:]
+                    raw = placed([P, PACK, N], F32, f"w2_raw{e}_{g}", W2_LAST_AT[g])
+                    nc.sync.dma_start(out=raw[:].rearrange("p j n -> p (j n)"), in_=w2_rows[:, g, :])
+                    w2_raw[e, g] = raw[:]
 
         windows = []
         for half in range(N_HALVES):
-            tile = held.tile([P, T], F32, name=f"window{half}")
-            nc.gpsimd.memset(tile[:], 0.0)
-            windows.append(tile)
+            window = held.tile([P, T], F32, name=f"window{half}")
+            nc.gpsimd.memset(window[:], 0.0)
+            windows.append(window)
 
         def copy_on(engine, dst, src):
             if engine == "vector":
                 nc.vector.tensor_copy(out=dst, in_=src)
             else:
                 nc.scalar.copy(out=dst, in_=src)
+
+        def interleave(engine, dst, src):
+            copy_on(
+                engine,
+                dst.rearrange("p (c r) j -> p c j r", r=RUN),
+                src.rearrange("p j (c r) -> p c j r", r=RUN),
+            )
 
         def quantize(src, words, name, bufs, place=None):
             if place is None:
@@ -117,79 +123,66 @@ def tile_moe_pre_mlp_silu_kernel(tc, xT, w1, w2, gate, offs, out):
             nc.vector.quantize_mx(out=codes[:].bitcast(FP8X4), scales=scales[:], in_=src)
             return codes, scales
 
+        def columns(quantised, first):
+            codes, scales = quantised
+            return codes[:, first : first + P], scales[:, first : first + P]
 
         x_bf = []
-        for c, engine in enumerate(X_ENGINES):
-            tile = stage.tile([P, CHUNK, PACK], BF16, name="x_bf", align_bytes=ALIGN, bufs=3)
-            copy_on(
-                engine,
-                tile[:].rearrange("p (c i) j -> p c j i", i=2),
-                gathered[:, :, c * CHUNK : (c + 1) * CHUNK].rearrange("p j (c i) -> p c j i", i=2),
-            )
-            x_bf.append(tile)
-        x_q = [quantize(tile[:].rearrange("p s j -> p (s j)"), CHUNK, "x", 3) for tile in x_bf]
+        for pair, engine in enumerate(X_ENGINES):
+            x_pair = stage.tile([P, X_SLOTS, PACK], BF16, name="x_bf", align_bytes=ALIGN, bufs=len(X_ENGINES))
+            interleave(engine, x_pair[:], gathered[:, :, pair * X_SLOTS : (pair + 1) * X_SLOTS])
+            x_bf.append(x_pair)
+        x_q = [quantize(x_pair[:].rearrange("p s j -> p (s j)"), X_SLOTS, "x", len(X_ENGINES)) for x_pair in x_bf]
 
         w1_bf = {}
-        w1_q = {}
-        w2_bf = {}
         w2_q = {}
         h_bf = {}
         h_q = {}
         y_acc = {}
         y_sb = {}
 
-        def cast_w1(e, g, shares):
-            tile = stage.tile([P, PACK, P, PACK], BF16, name="w1_bf", align_bytes=ALIGN, bufs=3)
-            src = w1_raw[e, g].rearrange("p j (m t) -> p m j t", t=PACK)
-            dst = tile[:].rearrange("p t m j -> p m j t")
+        def round_w1(e, g, shares):
+            rounded = stage.tile([P, PACK, P, PACK], BF16, name="w1_bf", align_bytes=ALIGN, bufs=3)
+            src = w1_raw[e, g].rearrange("p (u v) (m t) -> p m u t v", v=2, t=PACK)
+            dst = rounded[:].rearrange("p t m (u v) -> p m u t v", v=2)
             for engine, m0, m1 in shares:
-                if m1 > m0:
-                    copy_on(engine, dst[:, m0:m1, :, :], src[:, m0:m1, :, :])
-            w1_bf[e, g] = tile
-
-        def quantize_w1(e, g):
-            w1_q[e, g] = quantize(w1_bf[e, g][:].rearrange("p t m j -> p (t m j)"), K_PASS, "w1", 3)
+                copy_on(engine, dst[:, m0:m1, :, :, :], src[:, m0:m1, :, :, :])
+            w1_bf[e, g] = rounded
 
         def first_layer(e, g):
-            x_codes, x_scales = x_q[e // 2]
-            slots = slice((e % 2) * C, (e % 2 + 1) * C)
-            codes, scales = w1_q[e, g]
+            w1_q = quantize(w1_bf[e, g][:].rearrange("p t m j -> p (t m j)"), K_PASS, "w1", 3)
+            x_codes, x_scales = columns(x_q[e // 2], (e % 2) * C)
             acc = psum.tile([P, PACK, C], F32, name="acc1")
             for t in range(PACK):
-                m_cols = slice(t * P, (t + 1) * P)
+                w_codes, w_scales = columns(w1_q, t * P)
                 nc.tensor.matmul_mx(
                     out=acc[:, t, :],
-                    lhsT=codes[:, m_cols].bitcast(FP8X4),
-                    lhsT_scale=scales[:, m_cols],
-                    rhs=x_codes[:, slots].bitcast(FP8X4),
-                    rhs_scale=x_scales[:, slots],
+                    lhsT=w_codes.bitcast(FP8X4),
+                    lhsT_scale=w_scales,
+                    rhs=x_codes.bitcast(FP8X4),
+                    rhs_scale=x_scales,
                     start=True,
                     stop=True,
                 )
             return acc
 
         def silu(dst, acc):
-            nc.scalar.activation(out=dst, in_=acc[:].rearrange("p t c -> p c t"), func=SILU)
-
-        def cast_w2(e, tile, shares):
-            for engine, g, n0, n1 in shares:
-                if n1 > n0:
-                    copy_on(
-                        engine,
-                        tile[:, g, n0:n1, :].rearrange("p (c i) j -> p c j i", i=2),
-                        w2_raw[e, g][:, :, n0:n1].rearrange("p j (c i) -> p c j i", i=2),
-                    )
+            nc.scalar.activation(
+                out=dst.rearrange("p (c r) t -> p c t r", r=RUN),
+                in_=acc[:].rearrange("p t (c r) -> p c t r", r=RUN),
+                func=SILU,
+            )
 
         def second_layer(e, halves):
             acc = psum.tile([P, len(halves), C], F32, name="acc2")
-            for place, half in enumerate(halves):
+            for group, half in enumerate(halves):
                 for g in range(H_PASSES):
-                    codes, scales = w2_q[e, g, half]
+                    w_codes, w_scales = w2_q[e, g, half]
                     h_codes, h_scales = h_q[e, g]
                     nc.tensor.matmul_mx(
-                        out=acc[:, place, :],
-                        lhsT=codes.bitcast(FP8X4),
-                        lhsT_scale=scales,
+                        out=acc[:, group, :],
+                        lhsT=w_codes.bitcast(FP8X4),
+                        lhsT_scale=w_scales,
                         rhs=h_codes.bitcast(FP8X4),
                         rhs_scale=h_scales,
                         start=(g == 0),
@@ -197,116 +190,107 @@ def tile_moe_pre_mlp_silu_kernel(tc, xT, w1, w2, gate, offs, out):
                     )
             y_acc[e, halves] = acc
 
-        def leave_psum(c, e, halves, source):
-            s0, s1 = CHUNKS[c]
-            lo, hi = max(s0, e * C), min(s1, (e + 1) * C)
-            first = halves[0] - source[0]
-            tile, base = y_sb[c, halves[0]]
+        def finish_expert(e, place=None):
+            quantised = quantize(h_bf[e][:].rearrange("p g c t -> p (g c t)"), H_PASSES * C, "h", 2, place)
+            for g in range(H_PASSES):
+                h_q[e, g] = columns(quantised, g * C)
+            second_layer(e, BOTH)
+
+        def new_y(piece, halves, place):
+            y_tile = placed([P, len(halves), PIECE], F32, f"y_sb{piece}_{halves[0]}", place)
+            for half in halves:
+                y_sb[piece, half] = (y_tile, halves[0])
+
+        def leave_psum(piece, e, halves, acc_halves):
+            s0 = piece * PIECE
+            lo, hi = max(s0, e * C), min(s0 + PIECE, (e + 1) * C)
+            y_tile, y_first = y_sb[piece, halves[0]]
+            to, at = halves[0] - y_first, halves[0] - acc_halves[0]
             nc.scalar.copy(
-                out=tile[:, halves[0] - base : halves[-1] + 1 - base, lo - s0 : hi - s0],
-                in_=y_acc[e, source][:, first : first + len(halves), lo - e * C : hi - e * C],
+                out=y_tile[:, to : to + len(halves), lo - s0 : hi - s0],
+                in_=y_acc[e, acc_halves][:, at : at + len(halves), lo - e * C : hi - e * C],
             )
 
-        def scatter(c, half):
-            s0, s1 = CHUNKS[c]
-            tile, base = y_sb[c, half]
-            nc.vector.tensor_copy(windows[half][:].indirect(offsets[:, s0 // 16 : s1 // 16]), tile[:, half - base, :])
+        def collect_piece(piece, halves, place):
+            new_y(piece, halves, place)
+            for e in range(piece * PIECE // C, ((piece + 1) * PIECE - 1) // C + 1):
+                leave_psum(piece, e, halves, BOTH)
 
-        def y_tile(c, halves, place):
-            s0, s1 = CHUNKS[c]
-            tile = placed([P, len(halves), s1 - s0], F32, f"y_sb{c}_{halves[0]}", place)
-            for half in halves:
-                y_sb[c, half] = (tile, halves[0])
+        def scatter(piece, half):
+            y_tile, y_first = y_sb[piece, half]
+            entries = offsets[:, piece * PIECE // LIST_COLUMN : (piece + 1) * PIECE // LIST_COLUMN]
+            nc.vector.tensor_copy(windows[half][:].indirect(entries), y_tile[:, half - y_first, :])
 
-        def finish_chunk(c, halves, place):
-            s0, s1 = CHUNKS[c]
-            y_tile(c, halves, place)
-            for owner in range(s0 // C, (s1 - 1) // C + 1):
-                leave_psum(c, owner, halves, (0, 1))
-
-        def quantize_h(e, place):
-            codes, scales = quantize(h_bf[e][:].rearrange("p g c t -> p (g c t)"), H_PASSES * C, "h", 2, place)
-            for g in range(H_PASSES):
-                h_q[e, g] = (codes[:, g * C : (g + 1) * C], scales[:, g * C : (g + 1) * C])
-            second_layer(e, (0, 1))
-
-        for e in range(last):
-            cast_w1(e, 0, (("vector", 0, P),))
-            cast_w1(e, 1, (("scalar", V_W1[e] - P, P), ("vector", 0, V_W1[e] - P)))
-            accs = []
-            for g in range(H_PASSES):
-                quantize_w1(e, g)
-                accs.append(first_layer(e, g))
-            if e == 2 or (e == 3 and not DELAY_11):
-                finish_chunk(e - 2, (0, 1), e * W1_SLOT)
-                for half in range(N_HALVES):
-                    scatter(e - 2, half)
-            elif e >= 3 and DELAY_11:
-                finish_chunk(1, (e - 3,), e * W1_SLOT)
-                scatter(1, e - 3)
-            tile = stage.tile([P, H_PASSES, N, PACK], BF16, name="w2_bf", align_bytes=ALIGN)
-            cast_w2(e, tile, (("vector", 0, 0, V_W2[e]), ("scalar", 0, V_W2[e], N), ("scalar", 1, 0, N)))
-            h_bf[e] = placed([P, H_PASSES, C, PACK], BF16, f"h_bf{e}", W2_AT + e * W2_SLOT if e < last - 1 or H4_AT else e * W1_SLOT)
+        piece_beside = {2: 0, 3: 1}
+        for e in range(LAST):
+            round_w1(e, 0, (("vector", 0, P),))
+            round_w1(e, 1, (("scalar", V_W1[e], P), ("vector", 0, V_W1[e])))
+            accs = [first_layer(e, g) for g in range(H_PASSES)]
+            if e in piece_beside:
+                collect_piece(piece_beside[e], BOTH, e * W1_BYTES)
+                for half in BOTH:
+                    scatter(piece_beside[e], half)
+            w2_bf = stage.tile([P, H_PASSES, N, PACK], BF16, name="w2_bf", align_bytes=ALIGN)
+            for engine, g, n0, n1 in (("vector", 0, 0, V_W2[e]), ("scalar", 0, V_W2[e], N), ("scalar", 1, 0, N)):
+                if n1 > n0:
+                    interleave(engine, w2_bf[:, g, n0:n1, :], w2_raw[e, g][:, :, n0:n1])
+            h_bf[e] = placed([P, H_PASSES, C, PACK], BF16, f"h_bf{e}", W2_AT + e * W2_BYTES)
             for g in range(H_PASSES):
                 silu(h_bf[e][:, g, :, :], accs[g])
-            codes, scales = quantize(tile[:].rearrange("p g n j -> p (g n j)"), H_PASSES * N, "w2", 2)
+            quantised = quantize(w2_bf[:].rearrange("p g n j -> p (g n j)"), H_PASSES * N, "w2", 2)
             for g in range(H_PASSES):
-                for half in range(N_HALVES):
-                    m_cols = slice(g * N + half * P, g * N + (half + 1) * P)
-                    w2_q[e, g, half] = (codes[:, m_cols], scales[:, m_cols])
-            if e < last - 1:
-                quantize_h(e, None)
+                for half in BOTH:
+                    w2_q[e, g, half] = columns(quantised, g * N + half * P)
+            if e < LAST - 1:
+                finish_expert(e)
 
-        def quantize_h_last(g, h_tile):
-            codes, scales = quantize(h_tile[:].rearrange("p c t -> p (c t)"), C, "h_last", 2)
-            h_q[last, g] = (codes[:], scales[:])
+        w2_last_bf = []
 
-        cast_w1(last, 0, (("vector", 0, V_W1_LAST[0]), ("scalar", V_W1_LAST[0], P)))
-        quantize_h(last - 1, W1_LAST_AT[0] if QH4_AT else None)
-        quantize_w1(last, 0)
-        acc0 = first_layer(last, 0)
-        cast_w1(last, 1, (("vector", 0, V_W1_LAST[1]), ("scalar", V_W1_LAST[1], P)))
-        quantize_w1(last, 1)
-        acc1 = first_layer(last, 1)
-        finish_chunk(2, (0,), W1_LAST_AT[1])
-        h0 = placed([P, C, PACK], BF16, "h_last0", W1_LAST_AT[1] + KIB)
-        silu(h0[:], acc0)
+        def round_w1_last(g):
+            round_w1(LAST, g, (("vector", 0, V_W1_LAST[g]), ("scalar", V_W1_LAST[g], P)))
+
+        def silu_last(g, acc):
+            h_pass = placed([P, C, PACK], BF16, f"h_last{g}", W1_LAST_AT[1] + (1 + g) * KIB)
+            silu(h_pass[:], acc)
+            return h_pass
+
+        def quantize_h_last(g, h_pass):
+            h_q[LAST, g] = columns(quantize(h_pass[:].rearrange("p c t -> p (c t)"), C, "h_last", 2), 0)
+
+        def round_w2_last(g):
+            for half, engine in enumerate(("vector", "scalar")):
+                interleave(engine, w2_last_bf[half][:, g, :, :], w2_raw[LAST, g][:, :, half * P : (half + 1) * P])
+
+        def quantize_w2_last(half):
+            quantised = quantize(w2_last_bf[half][:].rearrange("p g n j -> p (g n j)"), H_PASSES * P, "w2_last", 2)
+            for g in range(H_PASSES):
+                w2_q[LAST, g, half] = columns(quantised, g * P)
+
+        round_w1_last(0)
+        finish_expert(LAST - 1, W1_LAST_AT[0])
+        acc_pass0 = first_layer(LAST, 0)
+        round_w1_last(1)
+        acc_pass1 = first_layer(LAST, 1)
+        collect_piece(2, (0,), W1_LAST_AT[1])
+        h_pass0 = silu_last(0, acc_pass0)
         scatter(2, 0)
-        quantize_h_last(0, h0)
-        halves_bf = [stage.tile([P, H_PASSES, P, PACK], BF16, name="w2_last_bf", align_bytes=ALIGN) for half in range(N_HALVES)]
-
-        def cast_last(engine, g, half):
-            copy_on(
-                engine,
-                halves_bf[half][:, g, :, :].rearrange("p (c i) j -> p c j i", i=2),
-                w2_raw[last, g][:, :, half * P : (half + 1) * P].rearrange("p j (c i) -> p c j i", i=2),
-            )
-
-        def quantize_last(half):
-            codes, scales = quantize(halves_bf[half][:].rearrange("p g n j -> p (g n j)"), N, "w2_last", 2)
-            for g in range(H_PASSES):
-                w2_q[last, g, half] = (codes[:, g * P : (g + 1) * P], scales[:, g * P : (g + 1) * P])
-
-        cast_last("vector" if V_B50 else "scalar", 0, 0)
-        cast_last("scalar", 0, 1)
-        h1 = placed([P, C, PACK], BF16, "h_last1", W2_LAST_AT[0] if H1_AT == 0 else W1_LAST_AT[1] + 2 * KIB)
-        silu(h1[:], acc1)
-        if Y21_AT == 0:
-            finish_chunk(2, (1,), W2_LAST_AT[0] + 3 * KIB)
-        cast_last("vector" if V_B51 else "scalar", 1, 0)
-        cast_last("vector" if V_B511 else "scalar", 1, 1)
-        quantize_h_last(1, h1)
-        quantize_last(0)
-        if Y21_AT == 1:
-            finish_chunk(2, (1,), W2_LAST_AT[1])
-        y_tile(3, (0, 1), W2_LAST_AT[1] + KIB)
-        leave_psum(3, last - 1, (0, 1), (0, 1))
-        second_layer(last, (0,))
-        leave_psum(3, last, (0,), (0,))
-        quantize_last(1)
+        quantize_h_last(0, h_pass0)
+        for half in BOTH:
+            w2_last_bf.append(stage.tile([P, H_PASSES, P, PACK], BF16, name="w2_last_bf", align_bytes=ALIGN))
+        round_w2_last(0)
+        h_pass1 = silu_last(1, acc_pass1)
+        round_w2_last(1)
+        quantize_h_last(1, h_pass1)
+        quantize_w2_last(0)
+        collect_piece(2, (1,), W2_LAST_AT[1])
+        new_y(3, BOTH, W2_LAST_AT[1] + KIB)
+        leave_psum(3, LAST - 1, BOTH, BOTH)
+        second_layer(LAST, (0,))
+        leave_psum(3, LAST, (0,), (0,))
+        quantize_w2_last(1)
         scatter(2, 1)
-        second_layer(last, (1,))
-        leave_psum(3, last, (1,), (1,))
-        for half in range(N_HALVES):
+        second_layer(LAST, (1,))
+        leave_psum(3, LAST, (1,), (1,))
+        for half in BOTH:
             scatter(3, half)
             nc.sync.dma_start(out=out[half * P : (half + 1) * P, :], in_=windows[half][:])

from contextlib import ExitStack

import concourse.mybir as mybir

K, T, E, C, H, N = 512, 1536, 6, 128, 1024, 256
S = E * C
FLOPS = 2 * S * (K * H + H * N)

F32 = mybir.dt.float32
BF16 = mybir.dt.bfloat16
U32 = mybir.dt.uint32
U16 = mybir.dt.uint16
U8 = mybir.dt.uint8
FP8X4 = mybir.dt.float8_e4m3fn_x4
MULT = mybir.AluOpType.mult
SILU = mybir.ActivationFunctionType.Silu

P = 128
PACK = 4
K_PASS = P * PACK
H_PASSES = H // K_PASS
N_HALVES = N // P
BOTH = (0, 1)
LAST = E - 1
LIST_COLUMN = 16
ALIGN = 64
RUN = 2

X_SLOTS = 2 * C
X_ENGINES = ("vector", "scalar", "vector")

PIECE = T // 8

V_W1 = (32, 32, 48, 32, 64)
V_W2 = (0, 128, 0, 0, 64)
V_W1_LAST = (112, 48)

KIB = 1024
W1_BYTES = 16 * KIB
W2_BYTES = 8 * KIB
GATE_AT = LAST * W1_BYTES
GATHERED_AT = GATE_AT + 12 * KIB
W1_LAST_AT = (GATE_AT, GATE_AT + 8 * KIB)
W2_LAST_AT = (GATE_AT + 16 * KIB, GATE_AT + 20 * KIB)
W2_AT = GATE_AT + 24 * KIB


def tile_moe_pre_mlp_silu_kernel(tc, xT, w1, w2, gate, offs, out):
    nc = tc.nc
    with ExitStack() as ctx:
        held = ctx.enter_context(tc.tile_pool(name="held", bufs=1))
        arena = ctx.enter_context(tc.tile_pool(name="arena", bufs=1))
        stage = ctx.enter_context(tc.tile_pool(name="stage", bufs=2))
        psum = ctx.enter_context(tc.psum_pool(name="psum", bufs=4))

        def placed(shape, dtype, name, place):
            return arena.tile(shape, dtype, name=name, align_bytes=ALIGN, offset=place)

        offsets = held.tile([P, S // LIST_COLUMN], U16, name="offsets")
        gate_sb = placed([P, PACK, S], F32, "gate_sb", GATE_AT)
        nc.sync.dma_start(out=gate_sb[:], in_=gate.rearrange("(p j) s -> p j s", j=PACK))
        nc.sync.dma_start(offsets[:], offs)
        x_rows = xT.rearrange("(p j) t -> p j t", j=PACK)
        x_sb = []
        for j in range(PACK):
            x_tile = held.tile([P, T], F32, name=f"x_sb{j}")
            nc.sync.dma_start(out=x_tile[:], in_=x_rows[:, j, :])
            x_sb.append(x_tile)

        gathered = placed([P, PACK, S], F32, "gathered", GATHERED_AT)
        for j in range(PACK):
            nc.vector.tensor_tensor(gathered[:, j, :], x_sb[j][:].indirect(offsets[:]), gate_sb[:, j, :], MULT)

        w1_raw = {}
        w2_raw = {}
        for e in range(E):
            w1_rows = w1[e].rearrange("(p j) i -> p j i", j=PACK)
            w2_rows = w2[e].rearrange("(g p j) n -> p g (j n)", g=H_PASSES, j=PACK)
            if e < LAST:
                raw = placed([P, PACK, H], F32, f"w1_raw{e}", e * W1_BYTES)
                nc.sync.dma_start(out=raw[:], in_=w1_rows)
                for g in range(H_PASSES):
                    w1_raw[e, g] = raw[:, :, g * K_PASS : (g + 1) * K_PASS]
                raw = placed([P, H_PASSES, PACK, N], F32, f"w2_raw{e}", W2_AT + e * W2_BYTES)
                nc.sync.dma_start(out=raw[:].rearrange("p g j n -> p g (j n)"), in_=w2_rows)
                for g in range(H_PASSES):
                    w2_raw[e, g] = raw[:, g, :, :]
            else:
                for g in range(H_PASSES):
                    raw = placed([P, PACK, K_PASS], F32, f"w1_raw{e}_{g}", W1_LAST_AT[g])
                    nc.sync.dma_start(out=raw[:], in_=w1_rows[:, :, g * K_PASS : (g + 1) * K_PASS])
                    w1_raw[e, g] = raw[:]
                for g in range(H_PASSES):
                    raw = placed([P, PACK, N], F32, f"w2_raw{e}_{g}", W2_LAST_AT[g])
                    nc.sync.dma_start(out=raw[:].rearrange("p j n -> p (j n)"), in_=w2_rows[:, g, :])
                    w2_raw[e, g] = raw[:]

        windows = []
        for half in range(N_HALVES):
            window = held.tile([P, T], F32, name=f"window{half}")
            nc.gpsimd.memset(window[:], 0.0)
            windows.append(window)

        def copy_on(engine, dst, src):
            if engine == "vector":
                nc.vector.tensor_copy(out=dst, in_=src)
            else:
                nc.scalar.copy(out=dst, in_=src)

        def interleave(engine, dst, src):
            copy_on(
                engine,
                dst.rearrange("p (c r) j -> p c j r", r=RUN),
                src.rearrange("p j (c r) -> p c j r", r=RUN),
            )

        def quantize(src, words, name, bufs, place=None):
            if place is None:
                codes = stage.tile([P, words], U32, name=name + "_codes", align_bytes=ALIGN, bufs=bufs)
            else:
                codes = placed([P, words], U32, name + "_placed_codes", place)
            scales = stage.tile([P, words], U8, name=name + "_scales", align_bytes=ALIGN, bufs=bufs)
            nc.vector.quantize_mx(out=codes[:].bitcast(FP8X4), scales=scales[:], in_=src)
            return codes, scales

        def columns(quantised, first):
            codes, scales = quantised
            return codes[:, first : first + P], scales[:, first : first + P]

        x_bf = []
        for pair, engine in enumerate(X_ENGINES):
            x_pair = stage.tile([P, X_SLOTS, PACK], BF16, name="x_bf", align_bytes=ALIGN, bufs=len(X_ENGINES))
            interleave(engine, x_pair[:], gathered[:, :, pair * X_SLOTS : (pair + 1) * X_SLOTS])
            x_bf.append(x_pair)
        x_q = [quantize(x_pair[:].rearrange("p s j -> p (s j)"), X_SLOTS, "x", len(X_ENGINES)) for x_pair in x_bf]

        w1_bf = {}
        w2_q = {}
        h_bf = {}
        h_q = {}
        y_acc = {}
        y_sb = {}

        def round_w1(e, g, shares):
            rounded = stage.tile([P, PACK, P, PACK], BF16, name="w1_bf", align_bytes=ALIGN, bufs=3)
            src = w1_raw[e, g].rearrange("p (u v) (m t) -> p m u t v", v=2, t=PACK)
            dst = rounded[:].rearrange("p t m (u v) -> p m u t v", v=2)
            for engine, m0, m1 in shares:
                copy_on(engine, dst[:, m0:m1, :, :, :], src[:, m0:m1, :, :, :])
            w1_bf[e, g] = rounded

        def first_layer(e, g):
            w1_q = quantize(w1_bf[e, g][:].rearrange("p t m j -> p (t m j)"), K_PASS, "w1", 3)
            x_codes, x_scales = columns(x_q[e // 2], (e % 2) * C)
            acc = psum.tile([P, PACK, C], F32, name="acc1")
            for t in range(PACK):
                w_codes, w_scales = columns(w1_q, t * P)
                nc.tensor.matmul_mx(
                    out=acc[:, t, :],
                    lhsT=w_codes.bitcast(FP8X4),
                    lhsT_scale=w_scales,
                    rhs=x_codes.bitcast(FP8X4),
                    rhs_scale=x_scales,
                    start=True,
                    stop=True,
                )
            return acc

        def silu(dst, acc):
            nc.scalar.activation(
                out=dst.rearrange("p (c r) t -> p c t r", r=RUN),
                in_=acc[:].rearrange("p t (c r) -> p c t r", r=RUN),
                func=SILU,
            )

        def second_layer(e, halves):
            acc = psum.tile([P, len(halves), C], F32, name="acc2")
            for group, half in enumerate(halves):
                for g in range(H_PASSES):
                    w_codes, w_scales = w2_q[e, g, half]
                    h_codes, h_scales = h_q[e, g]
                    nc.tensor.matmul_mx(
                        out=acc[:, group, :],
                        lhsT=w_codes.bitcast(FP8X4),
                        lhsT_scale=w_scales,
                        rhs=h_codes.bitcast(FP8X4),
                        rhs_scale=h_scales,
                        start=(g == 0),
                        stop=(g == H_PASSES - 1),
                    )
            y_acc[e, halves] = acc

        def finish_expert(e, place=None):
            quantised = quantize(h_bf[e][:].rearrange("p g c t -> p (g c t)"), H_PASSES * C, "h", 2, place)
            for g in range(H_PASSES):
                h_q[e, g] = columns(quantised, g * C)
            second_layer(e, BOTH)

        def new_y(piece, halves, place):
            y_tile = placed([P, len(halves), PIECE], F32, f"y_sb{piece}_{halves[0]}", place)
            for half in halves:
                y_sb[piece, half] = (y_tile, halves[0])

        def leave_psum(piece, e, halves, acc_halves):
            s0 = piece * PIECE
            lo, hi = max(s0, e * C), min(s0 + PIECE, (e + 1) * C)
            y_tile, y_first = y_sb[piece, halves[0]]
            to, at = halves[0] - y_first, halves[0] - acc_halves[0]
            nc.scalar.copy(
                out=y_tile[:, to : to + len(halves), lo - s0 : hi - s0],
                in_=y_acc[e, acc_halves][:, at : at + len(halves), lo - e * C : hi - e * C],
            )

        def collect_piece(piece, halves, place):
            new_y(piece, halves, place)
            for e in range(piece * PIECE // C, ((piece + 1) * PIECE - 1) // C + 1):
                leave_psum(piece, e, halves, BOTH)

        def scatter(piece, half):
            y_tile, y_first = y_sb[piece, half]
            entries = offsets[:, piece * PIECE // LIST_COLUMN : (piece + 1) * PIECE // LIST_COLUMN]
            nc.vector.tensor_copy(windows[half][:].indirect(entries), y_tile[:, half - y_first, :])

        piece_beside = {2: 0, 3: 1}
        for e in range(LAST):
            round_w1(e, 0, (("vector", 0, P),))
            round_w1(e, 1, (("scalar", V_W1[e], P), ("vector", 0, V_W1[e])))
            accs = [first_layer(e, g) for g in range(H_PASSES)]
            if e in piece_beside:
                collect_piece(piece_beside[e], BOTH, e * W1_BYTES)
                for half in BOTH:
                    scatter(piece_beside[e], half)
            w2_bf = stage.tile([P, H_PASSES, N, PACK], BF16, name="w2_bf", align_bytes=ALIGN)
            for engine, g, n0, n1 in (("vector", 0, 0, V_W2[e]), ("scalar", 0, V_W2[e], N), ("scalar", 1, 0, N)):
                if n1 > n0:
                    interleave(engine, w2_bf[:, g, n0:n1, :], w2_raw[e, g][:, :, n0:n1])
            h_bf[e] = placed([P, H_PASSES, C, PACK], BF16, f"h_bf{e}", W2_AT + e * W2_BYTES)
            for g in range(H_PASSES):
                silu(h_bf[e][:, g, :, :], accs[g])
            quantised = quantize(w2_bf[:].rearrange("p g n j -> p (g n j)"), H_PASSES * N, "w2", 2)
            for g in range(H_PASSES):
                for half in BOTH:
                    w2_q[e, g, half] = columns(quantised, g * N + half * P)
            if e < LAST - 1:
                finish_expert(e)

        w2_last_bf = []

        def round_w1_last(g):
            round_w1(LAST, g, (("vector", 0, V_W1_LAST[g]), ("scalar", V_W1_LAST[g], P)))

        def silu_last(g, acc):
            h_pass = placed([P, C, PACK], BF16, f"h_last{g}", W1_LAST_AT[1] + (1 + g) * KIB)
            silu(h_pass[:], acc)
            return h_pass

        def quantize_h_last(g, h_pass):
            h_q[LAST, g] = columns(quantize(h_pass[:].rearrange("p c t -> p (c t)"), C, "h_last", 2), 0)

        def round_w2_last(g):
            for half, engine in enumerate(("vector", "scalar")):
                interleave(engine, w2_last_bf[half][:, g, :, :], w2_raw[LAST, g][:, :, half * P : (half + 1) * P])

        def quantize_w2_last(half):
            quantised = quantize(w2_last_bf[half][:].rearrange("p g n j -> p (g n j)"), H_PASSES * P, "w2_last", 2)
            for g in range(H_PASSES):
                w2_q[LAST, g, half] = columns(quantised, g * P)

        round_w1_last(0)
        finish_expert(LAST - 1, W1_LAST_AT[0])
        acc_pass0 = first_layer(LAST, 0)
        round_w1_last(1)
        acc_pass1 = first_layer(LAST, 1)
        collect_piece(2, (0,), W1_LAST_AT[1])
        h_pass0 = silu_last(0, acc_pass0)
        scatter(2, 0)
        quantize_h_last(0, h_pass0)
        for half in BOTH:
            w2_last_bf.append(stage.tile([P, H_PASSES, P, PACK], BF16, name="w2_last_bf", align_bytes=ALIGN))
        round_w2_last(0)
        h_pass1 = silu_last(1, acc_pass1)
        round_w2_last(1)
        quantize_h_last(1, h_pass1)
        quantize_w2_last(0)
        collect_piece(2, (1,), W2_LAST_AT[1])
        new_y(3, BOTH, W2_LAST_AT[1] + KIB)
        leave_psum(3, LAST - 1, BOTH, BOTH)
        second_layer(LAST, (0,))
        leave_psum(3, LAST, (0,), (0,))
        quantize_w2_last(1)
        scatter(2, 1)
        second_layer(LAST, (1,))
        leave_psum(3, LAST, (1,), (1,))
        for half in BOTH:
            scatter(3, half)
            nc.sync.dma_start(out=out[half * P : (half + 1) * P, :], in_=windows[half][:])
